import numpy as np
CORES = [6,22,38,54,70,86,102,118]
N = 8
def setup_inputs(rng):
    return {"x": rng.standard_normal((N, 128, 256), dtype=np.float32)}
def reference(x):
    g = np.ascontiguousarray(x.transpose(1, 2, 0)).reshape(128, 256 * N)
    return {"y": np.broadcast_to(g, (N,) + g.shape)}

@@ -1,0 +1,96 @@
+from concourse.bass import DstId, RemoteDMATransfer
+
+FWD = (2, 3, 6, 7)
+
+SCRATCH = {
+    "xs": ("dram", [128, 128, 2], "float32"),
+    "inp": ("dram", [8, 128, 2], "float32"),
+    "il": ("dram", [128, 16], "float32"),
+    "fw": ("dram", [16, 128, 16], "float32"),
+    "yl": ("dram", [128, 128, 16], "float32"),
+}
+SEMAPHORES = ["loaded", "inp", "woven", "fw_a", "fw_b", "arr_even", "arr_odd", "own", "stored", "sent"]
+
+
+def rank_program(g, core, T, topo):
+    S = T.sem
+    ch, c = divmod(core, 8)
+    k, odd = divmod(ch, 2)
+    rank = T.rank_of(core)
+    row = 64 * odd + 8 * k + c
+    sent = 0
+
+    def row_of(w):
+        return 64 * ((w // 8) % 2) + 8 * (w // 16) + w % 8
+
+    def xfer(dst_core, engine, sem, src, dst):
+        a = topo.addr(dst_core)
+        return RemoteDMATransfer(dst_ids=[DstId(rid=a[0], pnc=a[1])], dma_engine_mask=1 << engine,
+                                 remote_sem=sem, src=src, dst=dst)
+
+    if rank is not None:
+        g.dma_start(T.xs[:], T.x[:]).then_inc(S.loaded, 16)
+        g.wait_ge(S.loaded, 16)
+        chips = [2 * ((k + d) % 8) + 1 for d in range(8)] + [2 * ((k + d) % 8) for d in range(1, 8)]
+        for n, dch in enumerate(chips):
+            ts = [xfer(8 * dch + cc, cc, S.inp, T.xs[row_of(8 * dch + cc)], T.inp[rank]) for cc in range(8)]
+            if n == 0:
+                ts += [xfer(8 * ch + cc, 8 + cc, S.inp, T.xs[row_of(8 * ch + cc)], T.inp[rank])
+                       for cc in range(8) if cc != c]
+            g.remote_dma_fused(ts, local_sem=S.sent)
+            sent += len(ts)
+
+    g.wait_ge(S.inp, 8 if rank is None else 7)
+    for r in range(8):
+        src = T.xs[row] if r == rank else T.inp[r]
+        g.dma_start(T.il[:, r::8], src, allow_slow_non_contiguous=True).then_inc(S.woven, 16)
+    g.wait_ge(S.woven, 8 * 16)
+
+    ts = []
+    eng = 0
+    if not odd:
+        for rc in T.cores:
+            if rc == core:
+                continue
+            if topo.chip(rc) == ch:
+                ts.append(xfer(rc, 8, S.arr_even, T.il[:], T.yl[row]))
+            else:
+                ts.append(xfer(rc, eng, S.arr_even, T.il[:], T.yl[row]))
+                eng += 1
+    else:
+        sem = S.fw_b if k % 2 else S.fw_a
+        for d in range(8):
+            fc = 8 * (2 * ((k + d) % 8) + 1) + FWD[k // 2]
+            if fc == core:
+                continue
+            if topo.chip(fc) == ch:
+                ts.append(xfer(fc, 8, sem, T.il[:], T.fw[8 * (k % 2) + c]))
+            else:
+                ts.append(xfer(fc, eng, sem, T.il[:], T.fw[8 * (k % 2) + c]))
+                eng += 1
+    g.remote_dma_fused(ts, local_sem=S.sent)
+    sent += len(ts)
+
+    if odd and c in FWD:
+        f = FWD.index(c)
+        mate_rank = 8 * (ch - 1) + 6
+        for half in range(2):
+            kk = 2 * f + half
+            g.wait_ge(S.fw_b if half else S.fw_a, 7 if kk == k else 8)
+            ts = [xfer(mate_rank, cc, S.arr_odd,
+                       T.il[:] if (kk == k and cc == c) else T.fw[8 * half + cc],
+                       T.yl[64 + 8 * kk + cc]) for cc in range(8)]
+            g.remote_dma_fused(ts, local_sem=S.sent)
+            sent += len(ts)
+
+    if rank is not None:
+        g.dma_start(T.y[row:row + 1, :], T.il[:]).then_inc(S.own, 16)
+        g.sync.wait_ge(S.arr_even, 63)
+        g.sync.dma_start(T.y[0:row, :], T.yl[0:row]).then_inc(S.stored, 16)
+        g.sync.dma_start(T.y[row + 1:64, :], T.yl[row + 1:64]).then_inc(S.stored, 16)
+        g.scalar.wait_ge(S.arr_odd, 64)
+        g.scalar.dma_start(T.y[64:128, :], T.yl[64:128]).then_inc(S.stored, 16)
+        g.wait_ge(S.own, 16)
+        g.wait_ge(S.stored, 48)
+
+    g.wait_ge(S.sent, sent)

@@ -9,7 +9,7 @@ SCRATCH = {
     "fw": ("dram", [16, 128, 16], "float32"),
     "yl": ("dram", [128, 128, 16], "float32"),
 }
-SEMAPHORES = ["loaded", "inp", "woven", "fw_a", "fw_b", "arr_even", "arr_odd", "own", "stored", "sent"]
+SEMAPHORES = ["loaded", "inp", "woven", "fw_a", "fw_b", "arr_even", "arr_a", "arr_b", "own", "stored", "sent"]
 
 
 def rank_program(g, core, T, topo):
@@ -58,15 +58,16 @@ def rank_program(g, core, T, topo):
                 ts.append(xfer(rc, eng, S.arr_even, T.il[:], T.yl[row]))
                 eng += 1
     else:
-        sem = S.fw_b if k % 2 else S.fw_a
+        half, f = divmod(k, 4)
+        sem = S.fw_b if half else S.fw_a
         for d in range(8):
-            fc = 8 * (2 * ((k + d) % 8) + 1) + FWD[k // 2]
+            fc = 8 * (2 * ((k + d) % 8) + 1) + FWD[f]
             if fc == core:
                 continue
             if topo.chip(fc) == ch:
-                ts.append(xfer(fc, 8, sem, T.il[:], T.fw[8 * (k % 2) + c]))
+                ts.append(xfer(fc, 8, sem, T.il[:], T.fw[8 * half + c]))
             else:
-                ts.append(xfer(fc, eng, sem, T.il[:], T.fw[8 * (k % 2) + c]))
+                ts.append(xfer(fc, eng, sem, T.il[:], T.fw[8 * half + c]))
                 eng += 1
     g.remote_dma_fused(ts, local_sem=S.sent)
     sent += len(ts)
@@ -75,9 +76,9 @@ def rank_program(g, core, T, topo):
         f = FWD.index(c)
         mate_rank = 8 * (ch - 1) + 6
         for half in range(2):
-            kk = 2 * f + half
+            kk = f + 4 * half
             g.wait_ge(S.fw_b if half else S.fw_a, 7 if kk == k else 8)
-            ts = [xfer(mate_rank, cc, S.arr_odd,
+            ts = [xfer(mate_rank, cc, S.arr_b if half else S.arr_a,
                        T.il[:] if (kk == k and cc == c) else T.fw[8 * half + cc],
                        T.yl[64 + 8 * kk + cc]) for cc in range(8)]
             g.remote_dma_fused(ts, local_sem=S.sent)
@@ -88,9 +89,11 @@ def rank_program(g, core, T, topo):
         g.sync.wait_ge(S.arr_even, 63)
         g.sync.dma_start(T.y[0:row, :], T.yl[0:row]).then_inc(S.stored, 16)
         g.sync.dma_start(T.y[row + 1:64, :], T.yl[row + 1:64]).then_inc(S.stored, 16)
-        g.scalar.wait_ge(S.arr_odd, 64)
-        g.scalar.dma_start(T.y[64:128, :], T.yl[64:128]).then_inc(S.stored, 16)
+        g.scalar.wait_ge(S.arr_a, 32)
+        g.scalar.dma_start(T.y[64:96, :], T.yl[64:96]).then_inc(S.stored, 16)
+        g.scalar.wait_ge(S.arr_b, 32)
+        g.scalar.dma_start(T.y[96:128, :], T.yl[96:128]).then_inc(S.stored, 16)
         g.wait_ge(S.own, 16)
-        g.wait_ge(S.stored, 48)
+        g.wait_ge(S.stored, 64)
 
     g.wait_ge(S.sent, sent)

from concourse.bass import DstId, RemoteDMATransfer

FWD = (2, 3, 6, 7)

SCRATCH = {
    "xs": ("dram", [128, 128, 2], "float32"),
    "inp": ("dram", [8, 128, 2], "float32"),
    "il": ("dram", [128, 16], "float32"),
    "fw": ("dram", [16, 128, 16], "float32"),
    "yl": ("dram", [128, 128, 16], "float32"),
}
SEMAPHORES = ["loaded", "inp", "woven", "fw_a", "fw_b", "arr_even", "arr_a", "arr_b", "own", "stored", "sent"]


def rank_program(g, core, T, topo):
    S = T.sem
    ch, c = divmod(core, 8)
    k, odd = divmod(ch, 2)
    rank = T.rank_of(core)
    row = 64 * odd + 8 * k + c
    sent = 0

    def row_of(w):
        return 64 * ((w // 8) % 2) + 8 * (w // 16) + w % 8

    def xfer(dst_core, engine, sem, src, dst):
        a = topo.addr(dst_core)
        return RemoteDMATransfer(dst_ids=[DstId(rid=a[0], pnc=a[1])], dma_engine_mask=1 << engine,
                                 remote_sem=sem, src=src, dst=dst)

    if rank is not None:
        g.dma_start(T.xs[:], T.x[:]).then_inc(S.loaded, 16)
        g.wait_ge(S.loaded, 16)
        chips = [2 * ((k + d) % 8) + 1 for d in range(8)] + [2 * ((k + d) % 8) for d in range(1, 8)]
        for n, dch in enumerate(chips):
            ts = [xfer(8 * dch + cc, cc, S.inp, T.xs[row_of(8 * dch + cc)], T.inp[rank]) for cc in range(8)]
            if n == 0:
                ts += [xfer(8 * ch + cc, 8 + cc, S.inp, T.xs[row_of(8 * ch + cc)], T.inp[rank])
                       for cc in range(8) if cc != c]
            g.remote_dma_fused(ts, local_sem=S.sent)
            sent += len(ts)

    g.wait_ge(S.inp, 8 if rank is None else 7)
    for r in range(8):
        src = T.xs[row] if r == rank else T.inp[r]
        g.dma_start(T.il[:, r::8], src, allow_slow_non_contiguous=True).then_inc(S.woven, 16)
    g.wait_ge(S.woven, 8 * 16)

    ts = []
    eng = 0
    if not odd:
        for rc in T.cores:
            if rc == core:
                continue
            if topo.chip(rc) == ch:
                ts.append(xfer(rc, 8, S.arr_even, T.il[:], T.yl[row]))
            else:
                ts.append(xfer(rc, eng, S.arr_even, T.il[:], T.yl[row]))
                eng += 1
    else:
        half, f = divmod(k, 4)
        sem = S.fw_b if half else S.fw_a
        for d in range(8):
            fc = 8 * (2 * ((k + d) % 8) + 1) + FWD[f]
            if fc == core:
                continue
            if topo.chip(fc) == ch:
                ts.append(xfer(fc, 8, sem, T.il[:], T.fw[8 * half + c]))
            else:
                ts.append(xfer(fc, eng, sem, T.il[:], T.fw[8 * half + c]))
                eng += 1
    g.remote_dma_fused(ts, local_sem=S.sent)
    sent += len(ts)

    if odd and c in FWD:
        f = FWD.index(c)
        mate_rank = 8 * (ch - 1) + 6
        for half in range(2):
            kk = f + 4 * half
            g.wait_ge(S.fw_b if half else S.fw_a, 7 if kk == k else 8)
            ts = [xfer(mate_rank, cc, S.arr_b if half else S.arr_a,
                       T.il[:] if (kk == k and cc == c) else T.fw[8 * half + cc],
                       T.yl[64 + 8 * kk + cc]) for cc in range(8)]
            g.remote_dma_fused(ts, local_sem=S.sent)
            sent += len(ts)

    if rank is not None:
        g.dma_start(T.y[row:row + 1, :], T.il[:]).then_inc(S.own, 16)
        g.sync.wait_ge(S.arr_even, 63)
        g.sync.dma_start(T.y[0:row, :], T.yl[0:row]).then_inc(S.stored, 16)
        g.sync.dma_start(T.y[row + 1:64, :], T.yl[row + 1:64]).then_inc(S.stored, 16)
        g.scalar.wait_ge(S.arr_a, 32)
        g.scalar.dma_start(T.y[64:96, :], T.yl[64:96]).then_inc(S.stored, 16)
        g.scalar.wait_ge(S.arr_b, 32)
        g.scalar.dma_start(T.y[96:128, :], T.yl[96:128]).then_inc(S.stored, 16)
        g.wait_ge(S.own, 16)
        g.wait_ge(S.stored, 64)

    g.wait_ge(S.sent, sent)
